import numpy as np
import ml_dtypes


def mxq(x, axis, fmt="e4m3"):
    dtype, down = {"e4m3": (ml_dtypes.float8_e4m3fn, 7), "e5m2": (ml_dtypes.float8_e5m2, 14)}[fmt]
    v = np.moveaxis(np.asarray(x, np.float32).astype(ml_dtypes.bfloat16).astype(np.float64), axis, -1)
    blocks = v.reshape(v.shape[:-1] + (-1, 32))
    amax = np.abs(blocks).max(-1, keepdims=True)
    byte = np.maximum(np.where(amax > 0, np.frexp(amax)[1] - 1 + 127, 0) - down, 1)
    scale = np.exp2(byte - 127.0)
    codes = (blocks / scale).astype(np.float32).astype(dtype).astype(np.float64)
    return np.moveaxis((codes * scale).reshape(v.shape), -1, axis)


WIDE = False


def mx_kscale(k):
    if not WIDE:
        return np.ones(k)
    levels = np.array([10, -10, 5, -5, 0])
    if k % 512:
        return np.exp2(np.random.permutation(np.resize(levels, k // 32))).repeat(32)
    a = np.empty((k // 512, 16))
    for p in range(k // 512):
        a[p, :8] = np.random.permutation(np.resize(levels, 8))
        for g in range(8):
            far = levels[np.abs(levels - a[p, g]) >= 10]
            a[p, g + 8] = far[np.random.randint(len(far))]
    return np.exp2(a.ravel()).repeat(32)


def f64(x):
    return np.asarray(x).astype(np.float64)


E2M1 = np.array([0.0, 0.5, 1.0, 1.5, 2.0, 3.0, 4.0, 6.0, -0.0, -0.5, -1.0, -1.5, -2.0, -3.0, -4.0, -6.0])


def pack_weight(w, fmt):
    k, n = w.shape
    w = f64(np.asarray(w, np.float32).astype(ml_dtypes.bfloat16)).reshape(k // 32, 32, n)
    amax = np.abs(w).max(1)
    if fmt == "e4m3":
        byte = np.frexp(amax)[1] - 1 + 127 - 7
    else:
        mant, ex = np.frexp(amax / 6.0)
        byte = np.where(mant > 0.5, ex, ex - 1) + 127
    byte = np.clip(np.where(amax > 0, byte, 1), 1, 254)
    scaled = (w * np.exp2(127.0 - byte)[:, None, :]).reshape(k, n).astype(np.float32)
    by_word = np.ascontiguousarray(scaled.reshape(k // 512, 128, 4, n).transpose(0, 1, 3, 2))
    if fmt == "e4m3":
        words = by_word.astype(ml_dtypes.float8_e4m3fn).view(np.uint8)
    else:
        c = by_word.astype(ml_dtypes.float4_e2m1fn).view(np.uint8) & 0xF
        words = (c[..., 0::2] | (c[..., 1::2] << 4)).reshape(k // 512, 128, 2 * n)
    return np.ascontiguousarray(words), np.ascontiguousarray(byte.astype(np.uint8).reshape(k // 512, 16, n))


def unpack_weight(words, scales, fmt):
    g, _, n = scales.shape
    words = np.ascontiguousarray(words).reshape(g, 128, n, -1)
    if fmt == "e4m3":
        vals = words.view(ml_dtypes.float8_e4m3fn).astype(np.float64)
    else:
        nib = np.empty((g, 128, n, 4), np.uint8)
        nib[..., 0::2] = words & 0xF
        nib[..., 1::2] = words >> 4
        vals = E2M1[nib]
    vals = vals * np.repeat(np.exp2(scales.astype(np.float64) - 127.0), 8, axis=1)[..., None]
    return vals.transpose(0, 1, 3, 2).reshape(g * 512, n)


K, M, T = 2048, 1024, 1024


def setup_inputs():
    n = np.random.standard_normal
    s = mx_kscale(K)[:, None]
    x = n((K, T)) * s
    x4 = pack_weight(x, "e2m1")
    rest = x - unpack_weight(*x4, "e2m1")
    p_w4 = pack_weight(n((K, M)) / np.sqrt(K) / s, "e2m1")
    return {
        "x4_words": x4[0],
        "x4_scales": x4[1],
        "xr": (rest).astype(np.float32),
        "w4_words": p_w4[0],
        "w4_scales": p_w4[1],
    }


def reference(x4_words, x4_scales, xr, w4_words, w4_scales):
    x4_ = unpack_weight(x4_words, x4_scales, "e2m1")
    xr_ = mxq(f64(xr), 0, "e4m3")
    w4_ = unpack_weight(w4_words, w4_scales, "e2m1")
    y = w4_.T @ x4_ + w4_.T @ xr_
    return np.maximum(y, 0.0) ** 2

@@ -1,0 +1,182 @@
+from contextlib import ExitStack
+
+import concourse.mybir as mybir
+
+K, M, T = 2048, 1024, 1024
+FLOPS = 2 * 2 * K * M * T
+
+F32 = mybir.dt.float32
+BF16 = mybir.dt.bfloat16
+I32 = mybir.dt.int32
+U32 = mybir.dt.uint32
+U8 = mybir.dt.uint8
+FP8X4 = mybir.dt.float8_e4m3fn_x4
+FP4X4 = mybir.dt.float4_e2m1fn_x4
+RELU = mybir.ActivationFunctionType.Relu
+SQUARE = mybir.ActivationFunctionType.Square
+
+P = 128
+K_PASS = 512
+PASSES = K // K_PASS
+N_TILES = M // P
+TH = 512
+EARLY = 5
+
+
+def tile_mix_xres_fm_relu2_kernel(tc, x4_words, x4_scales, xr, w4_words, w4_scales, out):
+    nc = tc.nc
+
+    with ExitStack() as ctx:
+        keep = ctx.enter_context(tc.tile_pool(name="keep", bufs=1))
+        grp_pool = ctx.enter_context(tc.tile_pool(name="grp", bufs=4))
+        res_pool = ctx.enter_context(tc.tile_pool(name="res", bufs=4))
+        psum = ctx.enter_context(tc.psum_pool(name="psum", bufs=1))
+        ctx.enter_context(tc.manual_schedule())
+
+        w_sc = [keep.tile([P, 1 + 2 * i, M], U8, name=f"w_sc{i}", align_bytes=256) for i in range(2)]
+        x_sc = [keep.tile([P, 1 + 2 * i, T], U8, name=f"x_sc{i}", align_bytes=256) for i in range(2)]
+        w0 = keep.tile([P, 2 * M], U8, name="w0", align_bytes=256)
+        w1 = keep.tile([P, 2 * M], U8, name="w1", align_bytes=256)
+        w23 = keep.tile([P, 2, 2 * M], U8, name="w23", align_bytes=256)
+        x0 = keep.tile([P, 2 * TH], U8, name="x0", align_bytes=256)
+        x123 = keep.tile([P, 3, 2 * TH], U8, name="x123", align_bytes=256)
+        xh1 = keep.tile([P, 4, 2 * TH], U8, name="xh1", align_bytes=256)
+        raw = [[keep.tile([P, 4, TH], F32, name=f"raw{h}{a}", align_bytes=256) for a in range(PASSES)] for h in range(2)]
+        codes = [[keep.tile([P, TH], U32, name=f"codes{h}{a}", align_bytes=256) for a in range(PASSES)] for h in range(2)]
+        r_sc = [[keep.tile([P, TH], U8, name=f"rsc{h}{a}", align_bytes=256) for a in range(PASSES)] for h in range(2)]
+        dummy = keep.tile([P, 8], F32, name="dummy")
+
+        def w_view(a, n):
+            if a < 2:
+                return (w0, w1)[a][:, 2 * P * n : 2 * P * (n + 1)].bitcast(FP4X4)
+            return w23[:, a - 2, 2 * P * n : 2 * P * (n + 1)].bitcast(FP4X4)
+
+        def w_scale(a, n):
+            return w_sc[min(a, 1)][:, max(a - 1, 0), P * n : P * (n + 1)]
+
+        def x_view(h, a):
+            if h:
+                return xh1[:, a, :].bitcast(FP4X4)
+            return (x0[:] if a == 0 else x123[:, a - 1, :]).bitcast(FP4X4)
+
+        def x_scale(h, a):
+            return x_sc[min(a, 1)][:, max(a - 1, 0), TH * h : TH * (h + 1)]
+
+        for i in range(2):
+            for t in (w_sc[i], x_sc[i]):
+                nc.vector.memset(t[:].rearrange("p a n -> p (a n)").bitcast(I32), 0)
+        nc.gpsimd.memset(dummy[:], 0.0)
+        def load_scales(eng, tile, src, pair, q):
+            eng.dma_start(
+                out=tile[32 * q : 32 * q + 4, :, :].bitcast(I32),
+                in_=src[pair : 1 + 3 * pair, 4 * q : 4 * q + 4, :].rearrange("a r n -> r a n").bitcast(I32),
+            )
+
+        nc.sync.dma_start(out=x0[:].bitcast(I32), in_=x4_words[0, :, 0 : 2 * TH].bitcast(I32))
+        nc.sync.dma_start(out=w0[:].bitcast(I32), in_=w4_words[0].bitcast(I32))
+        for q in range(4):
+            load_scales(nc.sync, w_sc[0], w4_scales, 0, q)
+            load_scales(nc.scalar, x_sc[0], x4_scales, 0, q)
+        nc.scalar.activation(out=dummy[:, 0:1], in_=dummy[:, 1:2], func=RELU)
+        for q in range(4):
+            load_scales(nc.sync, w_sc[1], w4_scales, 1, q)
+        for q in range(4):
+            load_scales(nc.sync, x_sc[1], x4_scales, 1, q)
+        nc.sync.dma_start(out=w1[:].bitcast(I32), in_=w4_words[1].bitcast(I32))
+        nc.sync.dma_start(
+            out=x123[:].bitcast(I32), in_=x4_words[1:4, :, 0 : 2 * TH].rearrange("a p b -> p a b").bitcast(I32)
+        )
+        nc.sync.dma_start(out=w23[:].bitcast(I32), in_=w4_words[2:4].rearrange("a p b -> p a b").bitcast(I32))
+
+        def load_xr(h, a):
+            nc.sync.dma_start(
+                out=raw[h][a][:],
+                in_=xr[K_PASS * a : K_PASS * (a + 1), TH * h : TH * (h + 1)].rearrange("(p j) t -> p j t", j=4),
+            )
+
+        for a in range(PASSES):
+            load_xr(0, a)
+        nc.sync.dma_start(
+            out=xh1[:].bitcast(I32), in_=x4_words[:, :, 2 * TH : 4 * TH].rearrange("a p b -> p a b").bitcast(I32)
+        )
+        for a in range(PASSES):
+            load_xr(1, a)
+
+        HALF = TH // 2
+        for h in range(2):
+            for a in range(PASSES):
+                parts = []
+                for c in range(2):
+                    g = grp_pool.tile([P, HALF, 4], BF16, name="g", align_bytes=256)
+                    nc.vector.tensor_copy(
+                        out=g[:], in_=raw[h][a][:, :, HALF * c : HALF * (c + 1)].rearrange("p j t -> p t j")
+                    )
+                    parts.append(g)
+                for c in range(2):
+                    nc.vector.quantize_mx(
+                        out=codes[h][a][:, HALF * c : HALF * (c + 1)].bitcast(FP8X4),
+                        scales=r_sc[h][a][:, HALF * c : HALF * (c + 1)],
+                        in_=parts[c][:].rearrange("p t j -> p (t j)"),
+                    )
+
+        def mm_x4(acc, n, h, a):
+            nc.tensor.matmul_mx(
+                out=acc[:], lhsT=w_view(a, n), lhsT_scale=w_scale(a, n), rhs=x_view(h, a), rhs_scale=x_scale(h, a),
+                start=(a == 0), stop=False,
+            )
+
+        def mm_xr(acc, n, h, a):
+            nc.tensor.matmul_mx(
+                out=acc[:], lhsT=w_view(a, n), lhsT_scale=w_scale(a, n),
+                rhs=codes[h][a][:].bitcast(FP8X4), rhs_scale=r_sc[h][a][:],
+                start=False, stop=(a == PASSES - 1),
+            )
+
+        def new_acc(h, n):
+            return psum.tile([P, TH], F32, name=f"acc{h}{n}", tag=f"bank{n}")
+
+        def finish_scalar(acc, h, n):
+            r = res_pool.tile([P, TH], F32, name="r0")
+            nc.scalar.activation(out=r[:], in_=acc[:], func=RELU)
+            o = res_pool.tile([P, TH], F32, name="o0", bufs=8)
+            nc.scalar.activation(out=o[:], in_=r[:], func=SQUARE)
+            nc.sync.dma_start(out=out[P * n : P * (n + 1), TH * h : TH * (h + 1)], in_=o[:])
+
+        def finish_both(acc, h, n, pieces=1):
+            w = TH // pieces
+            for c in range(pieces):
+                r = res_pool.tile([P, w], F32, name=f"r{pieces}")
+                nc.scalar.activation(out=r[:], in_=acc[:, w * c : w * (c + 1)], func=RELU)
+                o = res_pool.tile([P, w], F32, name=f"o{pieces}", bufs=8)
+                nc.vector.tensor_mul(out=o[:], in0=r[:], in1=r[:])
+                nc.sync.dma_start(
+                    out=out[P * n : P * (n + 1), TH * h + w * c : TH * h + w * (c + 1)], in_=o[:]
+                )
+
+        acc0 = [new_acc(0, n) for n in range(N_TILES)]
+        for a in range(PASSES):
+            for n in range(N_TILES):
+                mm_x4(acc0[n], n, 0, a)
+        for a in range(PASSES):
+            for n in range(N_TILES):
+                mm_xr(acc0[n], n, 0, a)
+        for n in range(N_TILES):
+            finish_scalar(acc0[n], 0, n)
+
+        acc1 = {}
+        for n in range(EARLY):
+            acc1[n] = new_acc(1, n)
+            for a in range(PASSES):
+                mm_x4(acc1[n], n, 1, a)
+        for a in range(PASSES):
+            for n in range(EARLY):
+                mm_xr(acc1[n], n, 1, a)
+        for n in range(EARLY):
+            finish_both(acc1[n], 1, n)
+        for n in range(EARLY, N_TILES):
+            acc = new_acc(1, n)
+            for a in range(PASSES):
+                mm_x4(acc, n, 1, a)
+            for a in range(PASSES):
+                mm_xr(acc, n, 1, a)
+            finish_both(acc, 1, n, pieces=2 if n == N_TILES - 1 else 1)

@@ -33,8 +33,8 @@ def tile_mix_xres_fm_relu2_kernel(tc, x4_words, x4_scales, xr, w4_words, w4_scal
         psum = ctx.enter_context(tc.psum_pool(name="psum", bufs=1))
         ctx.enter_context(tc.manual_schedule())
 
-        w_sc = [keep.tile([P, 1 + 2 * i, M], U8, name=f"w_sc{i}", align_bytes=256) for i in range(2)]
-        x_sc = [keep.tile([P, 1 + 2 * i, T], U8, name=f"x_sc{i}", align_bytes=256) for i in range(2)]
+        w_sc = keep.tile([P, PASSES, M], U8, name="w_sc", align_bytes=256)
+        x_sc = keep.tile([P, PASSES, T], U8, name="x_sc", align_bytes=256)
         w0 = keep.tile([P, 2 * M], U8, name="w0", align_bytes=256)
         w1 = keep.tile([P, 2 * M], U8, name="w1", align_bytes=256)
         w23 = keep.tile([P, 2, 2 * M], U8, name="w23", align_bytes=256)
@@ -52,7 +52,7 @@ def tile_mix_xres_fm_relu2_kernel(tc, x4_words, x4_scales, xr, w4_words, w4_scal
             return w23[:, a - 2, 2 * P * n : 2 * P * (n + 1)].bitcast(FP4X4)
 
         def w_scale(a, n):
-            return w_sc[min(a, 1)][:, max(a - 1, 0), P * n : P * (n + 1)]
+            return w_sc[:, a, P * n : P * (n + 1)]
 
         def x_view(h, a):
             if h:
@@ -60,28 +60,25 @@ def tile_mix_xres_fm_relu2_kernel(tc, x4_words, x4_scales, xr, w4_words, w4_scal
             return (x0[:] if a == 0 else x123[:, a - 1, :]).bitcast(FP4X4)
 
         def x_scale(h, a):
-            return x_sc[min(a, 1)][:, max(a - 1, 0), TH * h : TH * (h + 1)]
+            return x_sc[:, a, TH * h : TH * (h + 1)]
 
-        for i in range(2):
-            for t in (w_sc[i], x_sc[i]):
-                nc.vector.memset(t[:].rearrange("p a n -> p (a n)").bitcast(I32), 0)
-        nc.gpsimd.memset(dummy[:], 0.0)
-        def load_scales(eng, tile, src, pair, q):
-            eng.dma_start(
+        def load_scales(tile, src, q):
+            nc.sync.dma_start(
                 out=tile[32 * q : 32 * q + 4, :, :].bitcast(I32),
-                in_=src[pair : 1 + 3 * pair, 4 * q : 4 * q + 4, :].rearrange("a r n -> r a n").bitcast(I32),
+                in_=src[:, 4 * q : 4 * q + 4, :].rearrange("a r n -> r a n").bitcast(I32),
             )
+
+        for t in (w_sc, x_sc):
+            nc.vector.memset(t[:].rearrange("p a n -> p (a n)").bitcast(I32), 0)
+        nc.vector.memset(dummy[:], 0.0)
+        nc.scalar.activation(out=dummy[:, 0:1], in_=dummy[:, 1:2], func=RELU)
 
         nc.sync.dma_start(out=x0[:].bitcast(I32), in_=x4_words[0, :, 0 : 2 * TH].bitcast(I32))
         nc.sync.dma_start(out=w0[:].bitcast(I32), in_=w4_words[0].bitcast(I32))
-        for q in range(4):
-            load_scales(nc.sync, w_sc[0], w4_scales, 0, q)
-            load_scales(nc.scalar, x_sc[0], x4_scales, 0, q)
-        nc.scalar.activation(out=dummy[:, 0:1], in_=dummy[:, 1:2], func=RELU)
-        for q in range(4):
-            load_scales(nc.sync, w_sc[1], w4_scales, 1, q)
-        for q in range(4):
-            load_scales(nc.sync, x_sc[1], x4_scales, 1, q)
+        for q in (0, 2, 1, 3):
+            load_scales(w_sc, w4_scales, q)
+        for q in (0, 2, 1, 3):
+            load_scales(x_sc, x4_scales, q)
         nc.sync.dma_start(out=w1[:].bitcast(I32), in_=w4_words[1].bitcast(I32))
         nc.sync.dma_start(
             out=x123[:].bitcast(I32), in_=x4_words[1:4, :, 0 : 2 * TH].rearrange("a p b -> p a b").bitcast(I32)

@@ -21,6 +21,7 @@ PASSES = K // K_PASS
 N_TILES = M // P
 TH = 512
 EARLY = 5
+WARM = 5
 
 
 def tile_mix_xres_fm_relu2_kernel(tc, x4_words, x4_scales, xr, w4_words, w4_scales, out):
@@ -33,8 +34,9 @@ def tile_mix_xres_fm_relu2_kernel(tc, x4_words, x4_scales, xr, w4_words, w4_scal
         psum = ctx.enter_context(tc.psum_pool(name="psum", bufs=1))
         ctx.enter_context(tc.manual_schedule())
 
-        w_sc = keep.tile([P, PASSES, M], U8, name="w_sc", align_bytes=256)
-        x_sc = keep.tile([P, PASSES, T], U8, name="x_sc", align_bytes=256)
+        w_sc = [keep.tile([P, 2, M], U8, name=f"w_sc{i}", align_bytes=256) for i in range(2)]
+        x_sc = [keep.tile([P, 2, T], U8, name=f"x_sc{i}", align_bytes=256) for i in range(2)]
+        mixed = keep.tile([P, TH], U8, name="mixed", align_bytes=256)
         w0 = keep.tile([P, 2 * M], U8, name="w0", align_bytes=256)
         w1 = keep.tile([P, 2 * M], U8, name="w1", align_bytes=256)
         w23 = keep.tile([P, 2, 2 * M], U8, name="w23", align_bytes=256)
@@ -52,7 +54,7 @@ def tile_mix_xres_fm_relu2_kernel(tc, x4_words, x4_scales, xr, w4_words, w4_scal
             return w23[:, a - 2, 2 * P * n : 2 * P * (n + 1)].bitcast(FP4X4)
 
         def w_scale(a, n):
-            return w_sc[:, a, P * n : P * (n + 1)]
+            return w_sc[a // 2][:, a % 2, P * n : P * (n + 1)]
 
         def x_view(h, a):
             if h:
@@ -60,30 +62,16 @@ def tile_mix_xres_fm_relu2_kernel(tc, x4_words, x4_scales, xr, w4_words, w4_scal
             return (x0[:] if a == 0 else x123[:, a - 1, :]).bitcast(FP4X4)
 
         def x_scale(h, a):
-            return x_sc[:, a, TH * h : TH * (h + 1)]
+            return x_sc[a // 2][:, a % 2, TH * h : TH * (h + 1)]
 
-        def load_scales(tile, src, q):
+        def load_scales(tiles, src, pair, q):
             nc.sync.dma_start(
-                out=tile[32 * q : 32 * q + 4, :, :].bitcast(I32),
-                in_=src[:, 4 * q : 4 * q + 4, :].rearrange("a r n -> r a n").bitcast(I32),
+                out=tiles[pair][32 * q : 32 * q + 4, :, :].bitcast(I32),
+                in_=src[2 * pair : 2 * pair + 2, 4 * q : 4 * q + 4, :].rearrange("a r n -> r a n").bitcast(I32),
             )
 
-        for t in (w_sc, x_sc):
-            nc.vector.memset(t[:].rearrange("p a n -> p (a n)").bitcast(I32), 0)
-        nc.vector.memset(dummy[:], 0.0)
-        nc.scalar.activation(out=dummy[:, 0:1], in_=dummy[:, 1:2], func=RELU)
-
-        nc.sync.dma_start(out=x0[:].bitcast(I32), in_=x4_words[0, :, 0 : 2 * TH].bitcast(I32))
-        nc.sync.dma_start(out=w0[:].bitcast(I32), in_=w4_words[0].bitcast(I32))
-        for q in (0, 2, 1, 3):
-            load_scales(w_sc, w4_scales, q)
-        for q in (0, 2, 1, 3):
-            load_scales(x_sc, x4_scales, q)
-        nc.sync.dma_start(out=w1[:].bitcast(I32), in_=w4_words[1].bitcast(I32))
-        nc.sync.dma_start(
-            out=x123[:].bitcast(I32), in_=x4_words[1:4, :, 0 : 2 * TH].rearrange("a p b -> p a b").bitcast(I32)
-        )
-        nc.sync.dma_start(out=w23[:].bitcast(I32), in_=w4_words[2:4].rearrange("a p b -> p a b").bitcast(I32))
+        def zero(tile):
+            nc.vector.memset(tile[:].rearrange("p a n -> p (a n)").bitcast(I32), 0)
 
         def load_xr(h, a):
             nc.sync.dma_start(
@@ -91,6 +79,31 @@ def tile_mix_xres_fm_relu2_kernel(tc, x4_words, x4_scales, xr, w4_words, w4_scal
                 in_=xr[K_PASS * a : K_PASS * (a + 1), TH * h : TH * (h + 1)].rearrange("(p j) t -> p j t", j=4),
             )
 
+        QS = (0, 2, 1, 3)
+
+        nc.sync.dma_start(
+            out=mixed[:].bitcast(I32), in_=w4_scales.rearrange("a q (u c) -> (a q u) c", c=TH).bitcast(I32)
+        )
+        nc.sync.dma_start(out=x0[:].bitcast(I32), in_=x4_words[0, :, 0 : 2 * TH].bitcast(I32))
+        nc.sync.dma_start(out=w0[:].bitcast(I32), in_=w4_words[0].bitcast(I32))
+        for i in range(2):
+            zero(w_sc[i])
+            zero(x_sc[i])
+        nc.vector.memset(dummy[:], 0.0)
+        nc.scalar.activation(out=dummy[:, 0:1], in_=dummy[:, 1:2], func=RELU)
+        for q in QS:
+            load_scales(w_sc, w4_scales, 0, q)
+        for q in QS:
+            load_scales(x_sc, x4_scales, 0, q)
+        nc.sync.dma_start(out=w1[:].bitcast(I32), in_=w4_words[1].bitcast(I32))
+        nc.sync.dma_start(
+            out=x123[:].bitcast(I32), in_=x4_words[1:4, :, 0 : 2 * TH].rearrange("a p b -> p a b").bitcast(I32)
+        )
+        for q in QS:
+            load_scales(w_sc, w4_scales, 1, q)
+        for q in QS:
+            load_scales(x_sc, x4_scales, 1, q)
+        nc.sync.dma_start(out=w23[:].bitcast(I32), in_=w4_words[2:4].rearrange("a p b -> p a b").bitcast(I32))
         for a in range(PASSES):
             load_xr(0, a)
         nc.sync.dma_start(
@@ -98,6 +111,13 @@ def tile_mix_xres_fm_relu2_kernel(tc, x4_words, x4_scales, xr, w4_words, w4_scal
         )
         for a in range(PASSES):
             load_xr(1, a)
+
+        warm = psum.tile([P, TH], F32, name="warm", tag="bank7")
+        for i in range(WARM):
+            nc.tensor.matmul_mx(
+                out=warm[:], lhsT=w0[:, 0 : 2 * P].bitcast(FP4X4), lhsT_scale=mixed[:, 0:P],
+                rhs=x0[:].bitcast(FP4X4), rhs_scale=mixed[:], start=True, stop=True,
+            )
 
         HALF = TH // 2
         for h in range(2):

@@ -20,7 +20,7 @@ K_PASS = 512
 PASSES = K // K_PASS
 N_TILES = M // P
 TH = 512
-EARLY = 5
+EARLY = 6
 WARM = 5
 
 
@@ -125,11 +125,13 @@ def tile_mix_xres_fm_relu2_kernel(tc, x4_words, x4_scales, xr, w4_words, w4_scal
                 parts = []
                 for c in range(2):
                     g = grp_pool.tile([P, HALF, 4], BF16, name="g", align_bytes=256)
-                    nc.vector.tensor_copy(
-                        out=g[:], in_=raw[h][a][:, :, HALF * c : HALF * (c + 1)].rearrange("p j t -> p t j")
-                    )
+                    src = raw[h][a][:, :, HALF * c : HALF * (c + 1)].rearrange("p j t -> p t j")
+                    if h == 0 and c == 0:
+                        nc.scalar.copy(out=g[:], in_=src)
+                    else:
+                        nc.vector.tensor_copy(out=g[:], in_=src)
                     parts.append(g)
-                for c in range(2):
+                for c in (1, 0):
                     nc.vector.quantize_mx(
                         out=codes[h][a][:, HALF * c : HALF * (c + 1)].bitcast(FP8X4),
                         scales=r_sc[h][a][:, HALF * c : HALF * (c + 1)],

from contextlib import ExitStack

import concourse.mybir as mybir

K, M, T = 2048, 1024, 1024
FLOPS = 2 * 2 * K * M * T

F32 = mybir.dt.float32
BF16 = mybir.dt.bfloat16
I32 = mybir.dt.int32
U32 = mybir.dt.uint32
U8 = mybir.dt.uint8
FP8X4 = mybir.dt.float8_e4m3fn_x4
FP4X4 = mybir.dt.float4_e2m1fn_x4
RELU = mybir.ActivationFunctionType.Relu
SQUARE = mybir.ActivationFunctionType.Square

P = 128
K_PASS = 512
PASSES = K // K_PASS
N_TILES = M // P
TH = 512
EARLY = 6
WARM = 5


def tile_mix_xres_fm_relu2_kernel(tc, x4_words, x4_scales, xr, w4_words, w4_scales, out):
    nc = tc.nc

    with ExitStack() as ctx:
        keep = ctx.enter_context(tc.tile_pool(name="keep", bufs=1))
        grp_pool = ctx.enter_context(tc.tile_pool(name="grp", bufs=4))
        res_pool = ctx.enter_context(tc.tile_pool(name="res", bufs=4))
        psum = ctx.enter_context(tc.psum_pool(name="psum", bufs=1))
        ctx.enter_context(tc.manual_schedule())

        w_sc = [keep.tile([P, 2, M], U8, name=f"w_sc{i}", align_bytes=256) for i in range(2)]
        x_sc = [keep.tile([P, 2, T], U8, name=f"x_sc{i}", align_bytes=256) for i in range(2)]
        mixed = keep.tile([P, TH], U8, name="mixed", align_bytes=256)
        w0 = keep.tile([P, 2 * M], U8, name="w0", align_bytes=256)
        w1 = keep.tile([P, 2 * M], U8, name="w1", align_bytes=256)
        w23 = keep.tile([P, 2, 2 * M], U8, name="w23", align_bytes=256)
        x0 = keep.tile([P, 2 * TH], U8, name="x0", align_bytes=256)
        x123 = keep.tile([P, 3, 2 * TH], U8, name="x123", align_bytes=256)
        xh1 = keep.tile([P, 4, 2 * TH], U8, name="xh1", align_bytes=256)
        raw = [[keep.tile([P, 4, TH], F32, name=f"raw{h}{a}", align_bytes=256) for a in range(PASSES)] for h in range(2)]
        codes = [[keep.tile([P, TH], U32, name=f"codes{h}{a}", align_bytes=256) for a in range(PASSES)] for h in range(2)]
        r_sc = [[keep.tile([P, TH], U8, name=f"rsc{h}{a}", align_bytes=256) for a in range(PASSES)] for h in range(2)]
        dummy = keep.tile([P, 8], F32, name="dummy")

        def w_view(a, n):
            if a < 2:
                return (w0, w1)[a][:, 2 * P * n : 2 * P * (n + 1)].bitcast(FP4X4)
            return w23[:, a - 2, 2 * P * n : 2 * P * (n + 1)].bitcast(FP4X4)

        def w_scale(a, n):
            return w_sc[a // 2][:, a % 2, P * n : P * (n + 1)]

        def x_view(h, a):
            if h:
                return xh1[:, a, :].bitcast(FP4X4)
            return (x0[:] if a == 0 else x123[:, a - 1, :]).bitcast(FP4X4)

        def x_scale(h, a):
            return x_sc[a // 2][:, a % 2, TH * h : TH * (h + 1)]

        def load_scales(tiles, src, pair, q):
            nc.sync.dma_start(
                out=tiles[pair][32 * q : 32 * q + 4, :, :].bitcast(I32),
                in_=src[2 * pair : 2 * pair + 2, 4 * q : 4 * q + 4, :].rearrange("a r n -> r a n").bitcast(I32),
            )

        def zero(tile):
            nc.vector.memset(tile[:].rearrange("p a n -> p (a n)").bitcast(I32), 0)

        def load_xr(h, a):
            nc.sync.dma_start(
                out=raw[h][a][:],
                in_=xr[K_PASS * a : K_PASS * (a + 1), TH * h : TH * (h + 1)].rearrange("(p j) t -> p j t", j=4),
            )

        QS = (0, 2, 1, 3)

        nc.sync.dma_start(
            out=mixed[:].bitcast(I32), in_=w4_scales.rearrange("a q (u c) -> (a q u) c", c=TH).bitcast(I32)
        )
        nc.sync.dma_start(out=x0[:].bitcast(I32), in_=x4_words[0, :, 0 : 2 * TH].bitcast(I32))
        nc.sync.dma_start(out=w0[:].bitcast(I32), in_=w4_words[0].bitcast(I32))
        for i in range(2):
            zero(w_sc[i])
            zero(x_sc[i])
        nc.vector.memset(dummy[:], 0.0)
        nc.scalar.activation(out=dummy[:, 0:1], in_=dummy[:, 1:2], func=RELU)
        for q in QS:
            load_scales(w_sc, w4_scales, 0, q)
        for q in QS:
            load_scales(x_sc, x4_scales, 0, q)
        nc.sync.dma_start(out=w1[:].bitcast(I32), in_=w4_words[1].bitcast(I32))
        nc.sync.dma_start(
            out=x123[:].bitcast(I32), in_=x4_words[1:4, :, 0 : 2 * TH].rearrange("a p b -> p a b").bitcast(I32)
        )
        for q in QS:
            load_scales(w_sc, w4_scales, 1, q)
        for q in QS:
            load_scales(x_sc, x4_scales, 1, q)
        nc.sync.dma_start(out=w23[:].bitcast(I32), in_=w4_words[2:4].rearrange("a p b -> p a b").bitcast(I32))
        for a in range(PASSES):
            load_xr(0, a)
        nc.sync.dma_start(
            out=xh1[:].bitcast(I32), in_=x4_words[:, :, 2 * TH : 4 * TH].rearrange("a p b -> p a b").bitcast(I32)
        )
        for a in range(PASSES):
            load_xr(1, a)

        warm = psum.tile([P, TH], F32, name="warm", tag="bank7")
        for i in range(WARM):
            nc.tensor.matmul_mx(
                out=warm[:], lhsT=w0[:, 0 : 2 * P].bitcast(FP4X4), lhsT_scale=mixed[:, 0:P],
                rhs=x0[:].bitcast(FP4X4), rhs_scale=mixed[:], start=True, stop=True,
            )

        HALF = TH // 2
        for h in range(2):
            for a in range(PASSES):
                parts = []
                for c in range(2):
                    g = grp_pool.tile([P, HALF, 4], BF16, name="g", align_bytes=256)
                    src = raw[h][a][:, :, HALF * c : HALF * (c + 1)].rearrange("p j t -> p t j")
                    if h == 0 and c == 0:
                        nc.scalar.copy(out=g[:], in_=src)
                    else:
                        nc.vector.tensor_copy(out=g[:], in_=src)
                    parts.append(g)
                for c in (1, 0):
                    nc.vector.quantize_mx(
                        out=codes[h][a][:, HALF * c : HALF * (c + 1)].bitcast(FP8X4),
                        scales=r_sc[h][a][:, HALF * c : HALF * (c + 1)],
                        in_=parts[c][:].rearrange("p t j -> p (t j)"),
                    )

        def mm_x4(acc, n, h, a):
            nc.tensor.matmul_mx(
                out=acc[:], lhsT=w_view(a, n), lhsT_scale=w_scale(a, n), rhs=x_view(h, a), rhs_scale=x_scale(h, a),
                start=(a == 0), stop=False,
            )

        def mm_xr(acc, n, h, a):
            nc.tensor.matmul_mx(
                out=acc[:], lhsT=w_view(a, n), lhsT_scale=w_scale(a, n),
                rhs=codes[h][a][:].bitcast(FP8X4), rhs_scale=r_sc[h][a][:],
                start=False, stop=(a == PASSES - 1),
            )

        def new_acc(h, n):
            return psum.tile([P, TH], F32, name=f"acc{h}{n}", tag=f"bank{n}")

        def finish_scalar(acc, h, n):
            r = res_pool.tile([P, TH], F32, name="r0")
            nc.scalar.activation(out=r[:], in_=acc[:], func=RELU)
            o = res_pool.tile([P, TH], F32, name="o0", bufs=8)
            nc.scalar.activation(out=o[:], in_=r[:], func=SQUARE)
            nc.sync.dma_start(out=out[P * n : P * (n + 1), TH * h : TH * (h + 1)], in_=o[:])

        def finish_both(acc, h, n, pieces=1):
            w = TH // pieces
            for c in range(pieces):
                r = res_pool.tile([P, w], F32, name=f"r{pieces}")
                nc.scalar.activation(out=r[:], in_=acc[:, w * c : w * (c + 1)], func=RELU)
                o = res_pool.tile([P, w], F32, name=f"o{pieces}", bufs=8)
                nc.vector.tensor_mul(out=o[:], in0=r[:], in1=r[:])
                nc.sync.dma_start(
                    out=out[P * n : P * (n + 1), TH * h + w * c : TH * h + w * (c + 1)], in_=o[:]
                )

        acc0 = [new_acc(0, n) for n in range(N_TILES)]
        for a in range(PASSES):
            for n in range(N_TILES):
                mm_x4(acc0[n], n, 0, a)
        for a in range(PASSES):
            for n in range(N_TILES):
                mm_xr(acc0[n], n, 0, a)
        for n in range(N_TILES):
            finish_scalar(acc0[n], 0, n)

        acc1 = {}
        for n in range(EARLY):
            acc1[n] = new_acc(1, n)
            for a in range(PASSES):
                mm_x4(acc1[n], n, 1, a)
        for a in range(PASSES):
            for n in range(EARLY):
                mm_xr(acc1[n], n, 1, a)
        for n in range(EARLY):
            finish_both(acc1[n], 1, n)
        for n in range(EARLY, N_TILES):
            acc = new_acc(1, n)
            for a in range(PASSES):
                mm_x4(acc, n, 1, a)
            for a in range(PASSES):
                mm_xr(acc, n, 1, a)
            finish_both(acc, 1, n, pieces=2 if n == N_TILES - 1 else 1)
